import numpy as np
import ml_dtypes


def mxq(x, axis, fmt="e4m3"):
    dtype, down = {"e4m3": (ml_dtypes.float8_e4m3fn, 7), "e5m2": (ml_dtypes.float8_e5m2, 14)}[fmt]
    v = np.moveaxis(np.asarray(x, np.float32).astype(ml_dtypes.bfloat16).astype(np.float64), axis, -1)
    blocks = v.reshape(v.shape[:-1] + (-1, 32))
    amax = np.abs(blocks).max(-1, keepdims=True)
    byte = np.maximum(np.where(amax > 0, np.frexp(amax)[1] - 1 + 127, 0) - down, 1)
    scale = np.exp2(byte - 127.0)
    codes = (blocks / scale).astype(np.float32).astype(dtype).astype(np.float64)
    return np.moveaxis((codes * scale).reshape(v.shape), -1, axis)


WIDE = False


def mx_kscale(k):
    if not WIDE:
        return np.ones(k)
    levels = np.array([10, -10, 5, -5, 0])
    if k % 512:
        return np.exp2(np.random.permutation(np.resize(levels, k // 32))).repeat(32)
    a = np.empty((k // 512, 16))
    for p in range(k // 512):
        a[p, :8] = np.random.permutation(np.resize(levels, 8))
        for g in range(8):
            far = levels[np.abs(levels - a[p, g]) >= 10]
            a[p, g + 8] = far[np.random.randint(len(far))]
    return np.exp2(a.ravel()).repeat(32)


BF16 = ml_dtypes.bfloat16


def bf(x):
    return np.asarray(x, np.float32).astype(BF16)


def f64(x):
    return np.asarray(x).astype(np.float64)


E2M1 = np.array([0.0, 0.5, 1.0, 1.5, 2.0, 3.0, 4.0, 6.0, -0.0, -0.5, -1.0, -1.5, -2.0, -3.0, -4.0, -6.0])


def pack_weight(w, fmt):
    k, n = w.shape
    w = f64(bf(w)).reshape(k // 32, 32, n)
    amax = np.abs(w).max(1)
    if fmt == "e4m3":
        byte = np.frexp(amax)[1] - 1 + 127 - 7
    else:
        mant, ex = np.frexp(amax / 6.0)
        byte = np.where(mant > 0.5, ex, ex - 1) + 127
    byte = np.clip(np.where(amax > 0, byte, 1), 1, 254)
    scaled = (w * np.exp2(127.0 - byte)[:, None, :]).reshape(k, n).astype(np.float32)
    by_word = np.ascontiguousarray(scaled.reshape(k // 512, 128, 4, n).transpose(0, 1, 3, 2))
    if fmt == "e4m3":
        words = by_word.astype(ml_dtypes.float8_e4m3fn).view(np.uint8)
    else:
        c = by_word.astype(ml_dtypes.float4_e2m1fn).view(np.uint8) & 0xF
        words = c[..., 0::2] | (c[..., 1::2] << 4)
    return np.ascontiguousarray(words), np.ascontiguousarray(byte.astype(np.uint8).reshape(k // 512, 16, n))


def unpack_weight(words, scales, fmt):
    g, p, n, _ = words.shape
    if fmt == "e4m3":
        vals = np.ascontiguousarray(words).view(ml_dtypes.float8_e4m3fn).astype(np.float64)
    else:
        nib = np.empty((g, p, n, 4), np.uint8)
        nib[..., 0::2] = words & 0xF
        nib[..., 1::2] = words >> 4
        vals = E2M1[nib]
    vals = vals * np.repeat(np.exp2(scales.astype(np.float64) - 127.0), 8, axis=1)[..., None]
    return vals.transpose(0, 1, 3, 2).reshape(g * 512, n)
def pack4(w):
    words, scales = pack_weight(w, "e2m1")
    return words.reshape(words.shape[0], 128, -1), scales


def unpack4(words, scales):
    return unpack_weight(words.reshape(words.shape[0], 128, -1, 2), scales, "e2m1")


P, B, L, F, C = 2048, 512, 1024, 512, 1536

BLACK = 0.05
GAMMA = 1 / 2.2
MEAN = 0.1


def setup_inputs():
    s, t, u = mx_kscale(B), mx_kscale(L), mx_kscale(F)
    coef = (np.random.standard_normal((B, P)) + MEAN) * s[:, None]
    spectra = (np.random.standard_normal((B, L)) + MEAN) / np.sqrt(B) / L ** 0.25 / s[:, None] * t
    coef_words, coef_scales = pack4(coef)
    spectra_words, spectra_scales = pack4(spectra)
    return {"coef_words": coef_words,
            "coef_scales": coef_scales,
            "spectra_words": spectra_words,
            "spectra_scales": spectra_scales,
            "illum": bf(1 + 0.2 * np.random.standard_normal(L)),
            "sens": bf((np.random.standard_normal((L, F)) + MEAN) / L ** 0.25 / t[:, None] * u),
            "ccm": bf((np.random.standard_normal((F, C)) + MEAN) / np.sqrt(F) / u[:, None])}


def reference(coef_words, coef_scales, spectra_words, spectra_scales, illum, sens, ccm):
    coef = unpack4(coef_words, coef_scales)
    spectra = unpack4(spectra_words, spectra_scales)
    refl = coef.T @ spectra
    light = refl * f64(illum)
    resp = mxq(f64(sens), 1, "e4m3") @ mxq(f64(ccm), 0, "e4m3")
    linear = mxq(light, 1, "e4m3") @ mxq(resp, 0, "e4m3")
    return np.maximum(linear, BLACK) ** GAMMA

@@ -1,0 +1,302 @@
+from contextlib import ExitStack
+
+import concourse.mybir as mybir
+from concourse.masks import make_identity
+
+PIXELS, BASIS, WAVES, BANDS, CHANNELS = 2048, 512, 1024, 512, 1536
+BLACK = 0.05
+GAMMA = 1 / 2.2
+FLOPS = 2 * (PIXELS * BASIS * WAVES + WAVES * BANDS * CHANNELS + PIXELS * WAVES * CHANNELS)
+
+F32 = mybir.dt.float32
+BF16 = mybir.dt.bfloat16
+I32 = mybir.dt.int32
+U32 = mybir.dt.uint32
+U8 = mybir.dt.uint8
+FP8X4 = mybir.dt.float8_e4m3fn_x4
+FP4X4 = mybir.dt.float4_e2m1fn_x4
+ALU = mybir.AluOpType
+ACT = mybir.ActivationFunctionType
+
+P = 128
+SLOTS = 4
+BANK = 512
+GROUPS = WAVES // 512
+TILES = PIXELS // P
+CHUNKS = CHANNELS // BANK
+FIRST_ROUND = 6
+EARLY_TILES = 4
+HELPED = 4
+HELPED_LATE = 1
+
+
+def tile_spectral_camera_rendering_s12_kernel(
+    tc, coef_words, coef_scales, spectra_words, spectra_scales, illum, sens, ccm, out
+):
+    nc = tc.nc
+    with ExitStack() as ctx:
+        keep = ctx.enter_context(tc.tile_pool(name="keep", bufs=1))
+        psum = ctx.enter_context(tc.psum_pool(name="psum", bufs=4))
+        ctx.enter_context(tc.manual_schedule())
+
+        def kept(name, shape, dtype, tag=None, bufs=1):
+            return keep.tile(shape, dtype, name=name, tag=tag or name, bufs=bufs, align_bytes=64)
+
+        def bank(name, tag, shape, dtype=F32):
+            return psum.tile(shape, dtype, name=name, tag=tag)
+
+        spec_scale_raw = kept("spec_scale_raw", [P, WAVES], U8)
+        coef_scale = kept("coef_scale", [P, PIXELS], U8)
+        illum_rows = kept("illum_rows", [P, 2 * P], BF16)
+        ident_f32 = kept("ident_f32", [P, P], F32)
+        ident_bf16 = kept("ident_bf16", [P, P], BF16)
+        nc.vector.memset(spec_scale_raw[:].bitcast(I32), 0)
+        nc.vector.memset(illum_rows[:], 0.0)
+        nc.vector.memset(coef_scale[:].bitcast(I32), 0)
+
+        sens_raw = [kept("sens_raw%d" % k, [P, 2, BANDS], BF16) for k in range(4)]
+        ccm_raw = [kept("ccm_raw%d" % c, [P, SLOTS, BANK], BF16) for c in range(CHUNKS)]
+        spec_raw = kept("spec_raw", [P, 2 * WAVES], U8)
+        coef_early = kept("coef_early", [P, 2 * P * EARLY_TILES], U8)
+        coef_late = kept("coef_late", [P, 2 * P * (TILES - EARLY_TILES)], U8)
+
+        def load_sens(k):
+            g, h = divmod(k, 2)
+            rows = sens[512 * g : 512 * (g + 1), :].rearrange("(p j) f -> p j f", j=4)
+            nc.sync.dma_start(out=sens_raw[k][:], in_=rows[:, 2 * h : 2 * h + 2, :])
+
+        def load_ccm(c):
+            rows = ccm.rearrange("(p j) c -> p j c", j=SLOTS)
+            nc.sync.dma_start(out=ccm_raw[c][:], in_=rows[:, :, BANK * c : BANK * (c + 1)])
+
+        def load_scales(queue, plane, rows):
+            for quad in range(4):
+                queue.dma_start(
+                    out=plane[32 * quad : 32 * quad + 4, :].bitcast(I32),
+                    in_=rows[0, 4 * quad : 4 * quad + 4, :].bitcast(I32),
+                )
+
+        split = 2 * P * EARLY_TILES
+        nc.gpsimd.dma_start(
+            out=illum_rows[0:SLOTS, :].rearrange("t (b r) -> t b r", r=8),
+            in_=illum.rearrange("(b t r) -> t b r", t=SLOTS, r=8),
+        )
+        make_identity(nc, ident_bf16[:])
+        make_identity(nc, ident_f32[:])
+        load_scales(nc.sync, spec_scale_raw, spectra_scales)
+        load_ccm(0)
+        for k in range(4):
+            load_sens(k)
+        nc.sync.dma_start(out=spec_raw[:].bitcast(I32), in_=spectra_words[0].bitcast(I32))
+        nc.sync.dma_start(out=coef_early[:].bitcast(I32), in_=coef_words[0, :, 0:split].bitcast(I32))
+        load_scales(nc.sync, coef_scale, coef_scales)
+        load_ccm(1)
+        load_ccm(2)
+        nc.sync.dma_start(out=coef_late[:].bitcast(I32), in_=coef_words[0, :, split:].bitcast(I32))
+
+        def quantize(name, source, tag=None, bufs=1):
+            width = source.shape[1] // SLOTS
+            codes = kept(name + "_codes", [P, width], U32, tag and tag + "_codes", bufs)
+            scale = kept(name + "_scale", [P, width], U8, tag and tag + "_scale", bufs)
+            nc.vector.quantize_mx(out=codes[:].bitcast(FP8X4), scales=scale[:], in_=source)
+            return codes, scale
+
+        sens_t = [kept("sens_t%d" % g, [P, SLOTS * 512], BF16) for g in range(GROUPS)]
+        sens_mx = {}
+
+        def turn_sens(k):
+            g, h = divmod(k, 2)
+            turned = bank("sens_bank%d" % k, "a", [P, 4, P])
+            for j in range(2):
+                words = sens_raw[k][:, j, :].bitcast(F32)
+                for u in range(2):
+                    nc.tensor.transpose(turned[:, 2 * j + u, :], words[:, u : 2 * P : 2], ident_f32[:])
+            dst = sens_t[g][:].bitcast(F32).rearrange("p (t q a h x) -> p h t q a x", t=4, q=16, a=2, h=2)
+            nc.scalar.copy(out=dst[:, h], in_=turned[:].rearrange("p x (q t a) -> p t q a x", t=4, a=2))
+
+        def quantize_sens(g):
+            sens_mx[g] = quantize("sens%d" % g, sens_t[g][:])
+
+        ccm_il = {}
+        ccm_mx = {}
+
+        def interleave_ccm(c, copy):
+            ccm_il[c] = kept("ccm_il%d" % c, [P, BANK * SLOTS], BF16)
+            copy(
+                out=ccm_il[c][:].rearrange("p (n i j) -> p n j i", i=4, j=SLOTS),
+                in_=ccm_raw[c][:].rearrange("p j (n i) -> p n j i", i=4),
+            )
+
+        def quantize_ccm(c):
+            ccm_mx[c] = quantize("ccm%d" % c, ccm_il[c][:])
+
+        spec = kept("spec", [P, 2 * WAVES], U8)
+        spec_scale = kept("spec_scale", [P, WAVES], U8)
+        illum_full = kept("illum_full", [P, GROUPS, P, SLOTS], BF16)
+
+        def order_spectra(dst, src):
+            nc.vector.tensor_copy(
+                out=dst[:].bitcast(I32).rearrange("p (g t q w) -> p g t q w", g=GROUPS, t=SLOTS, q=16),
+                in_=src[:].bitcast(I32).rearrange("p (g q t w) -> p g t q w", g=GROUPS, t=SLOTS, q=16),
+            )
+
+        def spread_illum():
+            turned = bank("illum_bank", "a", [P, GROUPS, P], BF16)
+            for g in range(GROUPS):
+                nc.tensor.transpose(turned[:, g, :], illum_rows[:, P * g : P * (g + 1)], ident_bf16[:])
+            nc.scalar.copy(
+                out=illum_full[:],
+                in_=turned[:, :, 0:SLOTS].unsqueeze(2).to_broadcast([P, GROUPS, P, SLOTS]),
+            )
+
+        resp_bf = {}
+        resp_mx = {}
+
+        def resp_block(c, g, b):
+            if b == 0:
+                resp_bf[c, g] = kept("resp_bf%d_%d" % (c, g), [P, BANK * SLOTS], BF16, "resp_bf", 3)
+            acc = bank("resp_bank%d_%d_%d" % (c, g, b), "a", [P, SLOTS, P])
+            cols = slice(P * b, P * (b + 1))
+            for t in range(SLOTS):
+                waves = slice(P * t, P * (t + 1))
+                nc.tensor.matmul_mx(
+                    out=acc[:, t, :],
+                    lhsT=sens_mx[g][0][:, waves].bitcast(FP8X4),
+                    lhsT_scale=sens_mx[g][1][:, waves],
+                    rhs=ccm_mx[c][0][:, cols].bitcast(FP8X4),
+                    rhs_scale=ccm_mx[c][1][:, cols],
+                    start=True,
+                    stop=True,
+                )
+            dst = resp_bf[c, g][:, BANK * b : BANK * (b + 1)].rearrange("p (n t) -> p n t", t=SLOTS)
+            nc.scalar.copy(out=dst, in_=acc[:].rearrange("p t n -> p n t"))
+
+        def resp_group(c, g):
+            for b in range(4):
+                resp_block(c, g, b)
+
+        def quantize_resp(c, g):
+            resp_mx[c, g] = quantize("resp%d_%d" % (c, g), resp_bf[c, g][:])
+
+        light_bf = {}
+        light_mx = {}
+
+        def light_group(i, g, tag):
+            if g == 0:
+                light_bf[i] = kept("light_bf%d" % i, [P, GROUPS, P, SLOTS], BF16, "light_bf", 3)
+            acc = bank("refl_bank%d_%d" % (i, g), tag, [P, SLOTS, P])
+            source, first = (coef_early, i) if i < EARLY_TILES else (coef_late, i - EARLY_TILES)
+            for t in range(SLOTS):
+                at = P * (SLOTS * g + t)
+                nc.tensor.matmul_mx(
+                    out=acc[:, t, :],
+                    lhsT=spec[:, 2 * at : 2 * (at + P)].bitcast(FP4X4),
+                    lhsT_scale=spec_scale[:, at : at + P],
+                    rhs=source[:, 2 * P * first : 2 * P * (first + 1)].bitcast(FP4X4),
+                    rhs_scale=coef_scale[:, P * i : P * (i + 1)],
+                    start=(t == 0),
+                    stop=(t == SLOTS - 1),
+                )
+            nc.vector.tensor_tensor(
+                out=light_bf[i][:, g], in0=acc[:].rearrange("p t n -> p n t"), in1=illum_full[:, g], op=ALU.mult
+            )
+
+        def quantize_light(i):
+            light_mx[i] = quantize("light%d" % i, light_bf[i][:].rearrange("p g n t -> p (g n t)"))
+
+        result = [kept("result%d" % i, [P, CHANNELS], F32) for i in range(TILES)]
+
+        def linear(i, c, on_scalar=False):
+            acc = bank("lin_bank%d_%d" % (i, c), "a" if on_scalar else "b", [P, BANK])
+            for g in range(GROUPS):
+                nc.tensor.matmul_mx(
+                    out=acc[:],
+                    lhsT=light_mx[i][0][:, P * g : P * (g + 1)].bitcast(FP8X4),
+                    lhsT_scale=light_mx[i][1][:, P * g : P * (g + 1)],
+                    rhs=resp_mx[c, g][0][:].bitcast(FP8X4),
+                    rhs_scale=resp_mx[c, g][1][:],
+                    start=(g == 0),
+                    stop=(g == GROUPS - 1),
+                )
+            dst = result[i][:, BANK * c : BANK * (c + 1)]
+            if on_scalar:
+                nc.scalar.activation(out=dst, in_=acc[:], func=ACT.Relu, bias=-BLACK)
+            else:
+                nc.vector.tensor_scalar(
+                    out=dst, in0=acc[:], scalar1=BLACK, scalar2=0.0, op0=ALU.subtract, op1=ALU.max
+                )
+
+        def logarithm(i, cols):
+            nc.scalar.activation(out=result[i][:, cols], in_=result[i][:, cols], func=ACT.Ln, bias=BLACK)
+
+        def power(i, cols):
+            nc.scalar.activation(out=result[i][:, cols], in_=result[i][:, cols], func=ACT.Exp, scale=GAMMA)
+            nc.sync.dma_start(out=out[P * i : P * (i + 1), cols], in_=result[i][:, cols])
+
+        whole = slice(0, CHANNELS)
+        chunk = [slice(BANK * c, BANK * (c + 1)) for c in range(CHUNKS)]
+
+        order_spectra(spec_scale, spec_scale_raw)
+        spread_illum()
+        interleave_ccm(0, nc.vector.tensor_copy)
+        for k in range(4):
+            turn_sens(k)
+        quantize_ccm(0)
+        quantize_sens(0)
+        order_spectra(spec, spec_raw)
+        light_group(0, 0, "b")
+        quantize_sens(1)
+        resp_group(0, 0)
+        light_group(0, 1, "b")
+        resp_group(0, 1)
+        interleave_ccm(1, nc.vector.tensor_copy)
+        quantize_light(0)
+        quantize_ccm(1)
+        light_group(1, 0, "b")
+        light_group(1, 1, "b")
+        quantize_resp(0, 0)
+        resp_group(1, 0)
+        quantize_light(1)
+        interleave_ccm(2, nc.vector.tensor_copy)
+        quantize_resp(0, 1)
+        quantize_ccm(2)
+        pending = [(c, g) for c in range(1, CHUNKS) for g in range(GROUPS)]
+        for k, i in enumerate(range(2, FIRST_ROUND)):
+            light_group(i, 0, "b")
+            light_group(i, 1, "b")
+            if k + 1 < len(pending):
+                resp_group(*pending[k + 1])
+            else:
+                for j in range(HELPED):
+                    linear(j, 0, True)
+            if k < len(pending):
+                quantize_resp(*pending[k])
+            quantize_light(i)
+        for c in range(CHUNKS):
+            for i in range(FIRST_ROUND):
+                if c > 0 or i >= HELPED:
+                    linear(i, c)
+                logarithm(i, chunk[c])
+        light_group(FIRST_ROUND, 0, "a")
+        light_group(FIRST_ROUND, 1, "a")
+        quantize_light(FIRST_ROUND)
+        for i in range(FIRST_ROUND):
+            power(i, whole)
+        for i in range(FIRST_ROUND, TILES):
+            ahead = i + 1 < TILES
+            if ahead:
+                light_group(i + 1, 0, "a")
+                light_group(i + 1, 1, "a")
+            linear(i, 0)
+            if ahead:
+                quantize_light(i + 1)
+            linear(i, 1)
+            linear(i, 2, TILES - 1 - HELPED_LATE <= i < TILES - 1)
+            if ahead:
+                logarithm(i, whole)
+            else:
+                for c in range(CHUNKS):
+                    logarithm(i, chunk[c])
+        for i in range(FIRST_ROUND, TILES):
+            for cols in chunk if i in (FIRST_ROUND, TILES - 1) else [whole]:
+                power(i, cols)

@@ -27,7 +27,7 @@ CHUNKS = CHANNELS // BANK
 FIRST_ROUND = 6
 EARLY_TILES = 4
 HELPED = 4
-HELPED_LATE = 1
+HELPED_LATE = (14,)
 
 
 def tile_spectral_camera_rendering_s12_kernel(
@@ -50,10 +50,13 @@ def tile_spectral_camera_rendering_s12_kernel(
         illum_rows = kept("illum_rows", [P, 2 * P], BF16)
         ident_f32 = kept("ident_f32", [P, P], F32)
         ident_bf16 = kept("ident_bf16", [P, P], BF16)
-        nc.vector.memset(spec_scale_raw[:].bitcast(I32), 0)
         nc.vector.memset(illum_rows[:], 0.0)
+        nc.vector.memset(spec_scale_raw[:].bitcast(I32), 0)
         nc.vector.memset(coef_scale[:].bitcast(I32), 0)
 
+        warm = kept("warm", [P, 8], F32)
+        nc.vector.memset(warm[:], 1.0)
+        nc.scalar.activation(out=warm[:], in_=warm[:], func=ACT.Ln)
         sens_raw = [kept("sens_raw%d" % k, [P, 2, BANDS], BF16) for k in range(4)]
         ccm_raw = [kept("ccm_raw%d" % c, [P, SLOTS, BANK], BF16) for c in range(CHUNKS)]
         spec_raw = kept("spec_raw", [P, 2 * WAVES], U8)
@@ -77,20 +80,22 @@ def tile_spectral_camera_rendering_s12_kernel(
                 )
 
         split = 2 * P * EARLY_TILES
-        nc.gpsimd.dma_start(
+        make_identity(nc, ident_bf16[:])
+        make_identity(nc, ident_f32[:])
+        nc.sync.dma_start(
             out=illum_rows[0:SLOTS, :].rearrange("t (b r) -> t b r", r=8),
             in_=illum.rearrange("(b t r) -> t b r", t=SLOTS, r=8),
         )
-        make_identity(nc, ident_bf16[:])
-        make_identity(nc, ident_f32[:])
         load_scales(nc.sync, spec_scale_raw, spectra_scales)
+        load_sens(0)
+        load_sens(1)
         load_ccm(0)
-        for k in range(4):
-            load_sens(k)
+        load_sens(2)
+        load_sens(3)
+        load_ccm(1)
         nc.sync.dma_start(out=spec_raw[:].bitcast(I32), in_=spectra_words[0].bitcast(I32))
         nc.sync.dma_start(out=coef_early[:].bitcast(I32), in_=coef_words[0, :, 0:split].bitcast(I32))
         load_scales(nc.sync, coef_scale, coef_scales)
-        load_ccm(1)
         load_ccm(2)
         nc.sync.dma_start(out=coef_late[:].bitcast(I32), in_=coef_words[0, :, split:].bitcast(I32))
 
@@ -236,49 +241,45 @@ def tile_spectral_camera_rendering_s12_kernel(
         whole = slice(0, CHANNELS)
         chunk = [slice(BANK * c, BANK * (c + 1)) for c in range(CHUNKS)]
 
-        order_spectra(spec_scale, spec_scale_raw)
         spread_illum()
+        order_spectra(spec_scale, spec_scale_raw)
         interleave_ccm(0, nc.vector.tensor_copy)
-        for k in range(4):
-            turn_sens(k)
-        quantize_ccm(0)
+        turn_sens(0)
+        turn_sens(1)
+        turn_sens(2)
+        turn_sens(3)
         quantize_sens(0)
-        order_spectra(spec, spec_raw)
-        light_group(0, 0, "b")
-        quantize_sens(1)
+        quantize_ccm(0)
         resp_group(0, 0)
+        interleave_ccm(1, nc.vector.tensor_copy)
+        quantize_sens(1)
+        order_spectra(spec, spec_raw)
+        quantize_ccm(1)
+        light_group(0, 0, "b")
         light_group(0, 1, "b")
         resp_group(0, 1)
-        interleave_ccm(1, nc.vector.tensor_copy)
-        quantize_light(0)
-        quantize_ccm(1)
-        light_group(1, 0, "b")
-        light_group(1, 1, "b")
-        quantize_resp(0, 0)
-        resp_group(1, 0)
-        quantize_light(1)
         interleave_ccm(2, nc.vector.tensor_copy)
-        quantize_resp(0, 1)
+        quantize_light(0)
+        quantize_resp(0, 0)
         quantize_ccm(2)
-        pending = [(c, g) for c in range(1, CHUNKS) for g in range(GROUPS)]
-        for k, i in enumerate(range(2, FIRST_ROUND)):
+        pending = [(c, g) for c in range(CHUNKS) for g in range(GROUPS)]
+        for i in range(1, FIRST_ROUND):
             light_group(i, 0, "b")
             light_group(i, 1, "b")
-            if k + 1 < len(pending):
-                resp_group(*pending[k + 1])
+            if i + 1 < len(pending):
+                resp_group(*pending[i + 1])
             else:
                 for j in range(HELPED):
                     linear(j, 0, True)
-            if k < len(pending):
-                quantize_resp(*pending[k])
+            quantize_resp(*pending[i])
             quantize_light(i)
         for c in range(CHUNKS):
             for i in range(FIRST_ROUND):
                 if c > 0 or i >= HELPED:
                     linear(i, c)
                 logarithm(i, chunk[c])
-        light_group(FIRST_ROUND, 0, "a")
-        light_group(FIRST_ROUND, 1, "a")
+        light_group(FIRST_ROUND, 0, "b")
+        light_group(FIRST_ROUND, 1, "b")
         quantize_light(FIRST_ROUND)
         for i in range(FIRST_ROUND):
             power(i, whole)
@@ -291,7 +292,7 @@ def tile_spectral_camera_rendering_s12_kernel(
             if ahead:
                 quantize_light(i + 1)
             linear(i, 1)
-            linear(i, 2, TILES - 1 - HELPED_LATE <= i < TILES - 1)
+            linear(i, 2, i in HELPED_LATE)
             if ahead:
                 logarithm(i, whole)
             else:

@@ -27,7 +27,9 @@ CHUNKS = CHANNELS // BANK
 FIRST_ROUND = 6
 EARLY_TILES = 4
 HELPED = 4
-HELPED_LATE = (14,)
+FINE = 2
+LAST = [slice(0, 512), slice(512, 1024), slice(1024, 1536)]
+HELPED_LATE = (13,)
 
 
 def tile_spectral_camera_rendering_s12_kernel(
@@ -58,7 +60,8 @@ def tile_spectral_camera_rendering_s12_kernel(
         nc.vector.memset(warm[:], 1.0)
         nc.scalar.activation(out=warm[:], in_=warm[:], func=ACT.Ln)
         sens_raw = [kept("sens_raw%d" % k, [P, 2, BANDS], BF16) for k in range(4)]
-        ccm_raw = [kept("ccm_raw%d" % c, [P, SLOTS, BANK], BF16) for c in range(CHUNKS)]
+        pieces = [(0, 0, 256), (0, 256, 256), (1, 0, 512), (2, 0, 512)]
+        ccm_raw = [kept("ccm_raw%d" % k, [P, SLOTS, piece[2]], BF16) for k, piece in enumerate(pieces)]
         spec_raw = kept("spec_raw", [P, 2 * WAVES], U8)
         coef_early = kept("coef_early", [P, 2 * P * EARLY_TILES], U8)
         coef_late = kept("coef_late", [P, 2 * P * (TILES - EARLY_TILES)], U8)
@@ -68,9 +71,10 @@ def tile_spectral_camera_rendering_s12_kernel(
             rows = sens[512 * g : 512 * (g + 1), :].rearrange("(p j) f -> p j f", j=4)
             nc.sync.dma_start(out=sens_raw[k][:], in_=rows[:, 2 * h : 2 * h + 2, :])
 
-        def load_ccm(c):
+        def load_ccm(k):
+            c, first, width = pieces[k]
             rows = ccm.rearrange("(p j) c -> p j c", j=SLOTS)
-            nc.sync.dma_start(out=ccm_raw[c][:], in_=rows[:, :, BANK * c : BANK * (c + 1)])
+            nc.sync.dma_start(out=ccm_raw[k][:], in_=rows[:, :, BANK * c + first : BANK * c + first + width])
 
         def load_scales(queue, plane, rows):
             for quad in range(4):
@@ -86,17 +90,18 @@ def tile_spectral_camera_rendering_s12_kernel(
             out=illum_rows[0:SLOTS, :].rearrange("t (b r) -> t b r", r=8),
             in_=illum.rearrange("(b t r) -> t b r", t=SLOTS, r=8),
         )
-        load_scales(nc.sync, spec_scale_raw, spectra_scales)
         load_sens(0)
-        load_sens(1)
         load_ccm(0)
+        load_sens(1)
+        load_ccm(1)
         load_sens(2)
         load_sens(3)
-        load_ccm(1)
+        load_ccm(2)
         nc.sync.dma_start(out=spec_raw[:].bitcast(I32), in_=spectra_words[0].bitcast(I32))
         nc.sync.dma_start(out=coef_early[:].bitcast(I32), in_=coef_words[0, :, 0:split].bitcast(I32))
+        load_scales(nc.sync, spec_scale_raw, spectra_scales)
         load_scales(nc.sync, coef_scale, coef_scales)
-        load_ccm(2)
+        load_ccm(3)
         nc.sync.dma_start(out=coef_late[:].bitcast(I32), in_=coef_words[0, :, split:].bitcast(I32))
 
         def quantize(name, source, tag=None, bufs=1):
@@ -125,11 +130,14 @@ def tile_spectral_camera_rendering_s12_kernel(
         ccm_il = {}
         ccm_mx = {}
 
-        def interleave_ccm(c, copy):
-            ccm_il[c] = kept("ccm_il%d" % c, [P, BANK * SLOTS], BF16)
-            copy(
-                out=ccm_il[c][:].rearrange("p (n i j) -> p n j i", i=4, j=SLOTS),
-                in_=ccm_raw[c][:].rearrange("p j (n i) -> p n j i", i=4),
+        def interleave_ccm(k):
+            c, first, width = pieces[k]
+            if first == 0:
+                ccm_il[c] = kept("ccm_il%d" % c, [P, BANK * SLOTS], BF16)
+            dst = ccm_il[c][:, SLOTS * first : SLOTS * (first + width)]
+            nc.vector.tensor_copy(
+                out=dst.rearrange("p (n i j) -> p n j i", i=4, j=SLOTS),
+                in_=ccm_raw[k][:].rearrange("p j (n i) -> p n j i", i=4),
             )
 
         def quantize_ccm(c):
@@ -242,8 +250,8 @@ def tile_spectral_camera_rendering_s12_kernel(
         chunk = [slice(BANK * c, BANK * (c + 1)) for c in range(CHUNKS)]
 
         spread_illum()
-        order_spectra(spec_scale, spec_scale_raw)
-        interleave_ccm(0, nc.vector.tensor_copy)
+        interleave_ccm(0)
+        interleave_ccm(1)
         turn_sens(0)
         turn_sens(1)
         turn_sens(2)
@@ -251,14 +259,18 @@ def tile_spectral_camera_rendering_s12_kernel(
         quantize_sens(0)
         quantize_ccm(0)
         resp_group(0, 0)
-        interleave_ccm(1, nc.vector.tensor_copy)
+        interleave_ccm(2)
         quantize_sens(1)
+        order_spectra(spec_scale, spec_scale_raw)
         order_spectra(spec, spec_raw)
         quantize_ccm(1)
+        resp_block(0, 1, 0)
+        resp_block(0, 1, 1)
         light_group(0, 0, "b")
         light_group(0, 1, "b")
-        resp_group(0, 1)
-        interleave_ccm(2, nc.vector.tensor_copy)
+        resp_block(0, 1, 2)
+        resp_block(0, 1, 3)
+        interleave_ccm(3)
         quantize_light(0)
         quantize_resp(0, 0)
         quantize_ccm(2)
@@ -280,24 +292,23 @@ def tile_spectral_camera_rendering_s12_kernel(
                 logarithm(i, chunk[c])
         light_group(FIRST_ROUND, 0, "b")
         light_group(FIRST_ROUND, 1, "b")
+        light_group(FIRST_ROUND + 1, 0, "b")
         quantize_light(FIRST_ROUND)
+        light_group(FIRST_ROUND + 1, 1, "b")
         for i in range(FIRST_ROUND):
             power(i, whole)
         for i in range(FIRST_ROUND, TILES):
-            ahead = i + 1 < TILES
-            if ahead:
-                light_group(i + 1, 0, "a")
-                light_group(i + 1, 1, "a")
+            if i + 2 < TILES:
+                light_group(i + 2, 0, "a")
             linear(i, 0)
-            if ahead:
+            if i + 1 < TILES:
                 quantize_light(i + 1)
+            if i + 2 < TILES:
+                light_group(i + 2, 1, "a")
             linear(i, 1)
             linear(i, 2, i in HELPED_LATE)
-            if ahead:
-                logarithm(i, whole)
-            else:
-                for c in range(CHUNKS):
-                    logarithm(i, chunk[c])
+            for cols in chunk if i >= TILES - FINE else [whole]:
+                logarithm(i, cols)
         for i in range(FIRST_ROUND, TILES):
-            for cols in chunk if i in (FIRST_ROUND, TILES - 1) else [whole]:
+            for cols in chunk if i == FIRST_ROUND else (LAST if i == TILES - 1 else [whole]):
                 power(i, cols)

@@ -26,7 +26,7 @@ TILES = PIXELS // P
 CHUNKS = CHANNELS // BANK
 FIRST_ROUND = 6
 EARLY_TILES = 4
-HELPED = 4
+HELPED = 3
 FINE = 2
 LAST = [slice(0, 512), slice(512, 1024), slice(1024, 1536)]
 HELPED_LATE = (13,)
@@ -60,8 +60,7 @@ def tile_spectral_camera_rendering_s12_kernel(
         nc.vector.memset(warm[:], 1.0)
         nc.scalar.activation(out=warm[:], in_=warm[:], func=ACT.Ln)
         sens_raw = [kept("sens_raw%d" % k, [P, 2, BANDS], BF16) for k in range(4)]
-        pieces = [(0, 0, 256), (0, 256, 256), (1, 0, 512), (2, 0, 512)]
-        ccm_raw = [kept("ccm_raw%d" % k, [P, SLOTS, piece[2]], BF16) for k, piece in enumerate(pieces)]
+        ccm_raw = [kept("ccm_raw%d" % c, [P, SLOTS, BANK], BF16) for c in range(CHUNKS)]
         spec_raw = kept("spec_raw", [P, 2 * WAVES], U8)
         coef_early = kept("coef_early", [P, 2 * P * EARLY_TILES], U8)
         coef_late = kept("coef_late", [P, 2 * P * (TILES - EARLY_TILES)], U8)
@@ -71,10 +70,9 @@ def tile_spectral_camera_rendering_s12_kernel(
             rows = sens[512 * g : 512 * (g + 1), :].rearrange("(p j) f -> p j f", j=4)
             nc.sync.dma_start(out=sens_raw[k][:], in_=rows[:, 2 * h : 2 * h + 2, :])
 
-        def load_ccm(k):
-            c, first, width = pieces[k]
+        def load_ccm(c):
             rows = ccm.rearrange("(p j) c -> p j c", j=SLOTS)
-            nc.sync.dma_start(out=ccm_raw[k][:], in_=rows[:, :, BANK * c + first : BANK * c + first + width])
+            nc.sync.dma_start(out=ccm_raw[c][:], in_=rows[:, :, BANK * c : BANK * (c + 1)])
 
         def load_scales(queue, plane, rows):
             for quad in range(4):
@@ -90,18 +88,17 @@ def tile_spectral_camera_rendering_s12_kernel(
             out=illum_rows[0:SLOTS, :].rearrange("t (b r) -> t b r", r=8),
             in_=illum.rearrange("(b t r) -> t b r", t=SLOTS, r=8),
         )
+        load_scales(nc.gpsimd, spec_scale_raw, spectra_scales)
         load_sens(0)
-        load_ccm(0)
         load_sens(1)
-        load_ccm(1)
+        load_ccm(0)
         load_sens(2)
         load_sens(3)
-        load_ccm(2)
+        load_ccm(1)
         nc.sync.dma_start(out=spec_raw[:].bitcast(I32), in_=spectra_words[0].bitcast(I32))
         nc.sync.dma_start(out=coef_early[:].bitcast(I32), in_=coef_words[0, :, 0:split].bitcast(I32))
-        load_scales(nc.sync, spec_scale_raw, spectra_scales)
         load_scales(nc.sync, coef_scale, coef_scales)
-        load_ccm(3)
+        load_ccm(2)
         nc.sync.dma_start(out=coef_late[:].bitcast(I32), in_=coef_words[0, :, split:].bitcast(I32))
 
         def quantize(name, source, tag=None, bufs=1):
@@ -130,14 +127,11 @@ def tile_spectral_camera_rendering_s12_kernel(
         ccm_il = {}
         ccm_mx = {}
 
-        def interleave_ccm(k):
-            c, first, width = pieces[k]
-            if first == 0:
-                ccm_il[c] = kept("ccm_il%d" % c, [P, BANK * SLOTS], BF16)
-            dst = ccm_il[c][:, SLOTS * first : SLOTS * (first + width)]
-            nc.vector.tensor_copy(
-                out=dst.rearrange("p (n i j) -> p n j i", i=4, j=SLOTS),
-                in_=ccm_raw[k][:].rearrange("p j (n i) -> p n j i", i=4),
+        def interleave_ccm(c, copy):
+            ccm_il[c] = kept("ccm_il%d" % c, [P, BANK * SLOTS], BF16)
+            copy(
+                out=ccm_il[c][:].rearrange("p (n i j) -> p n j i", i=4, j=SLOTS),
+                in_=ccm_raw[c][:].rearrange("p j (n i) -> p n j i", i=4),
             )
 
         def quantize_ccm(c):
@@ -250,8 +244,7 @@ def tile_spectral_camera_rendering_s12_kernel(
         chunk = [slice(BANK * c, BANK * (c + 1)) for c in range(CHUNKS)]
 
         spread_illum()
-        interleave_ccm(0)
-        interleave_ccm(1)
+        interleave_ccm(0, nc.vector.tensor_copy)
         turn_sens(0)
         turn_sens(1)
         turn_sens(2)
@@ -259,18 +252,15 @@ def tile_spectral_camera_rendering_s12_kernel(
         quantize_sens(0)
         quantize_ccm(0)
         resp_group(0, 0)
-        interleave_ccm(2)
+        interleave_ccm(1, nc.vector.tensor_copy)
         quantize_sens(1)
         order_spectra(spec_scale, spec_scale_raw)
         order_spectra(spec, spec_raw)
         quantize_ccm(1)
-        resp_block(0, 1, 0)
-        resp_block(0, 1, 1)
         light_group(0, 0, "b")
         light_group(0, 1, "b")
-        resp_block(0, 1, 2)
-        resp_block(0, 1, 3)
-        interleave_ccm(3)
+        resp_group(0, 1)
+        interleave_ccm(2, nc.vector.tensor_copy)
         quantize_light(0)
         quantize_resp(0, 0)
         quantize_ccm(2)

from contextlib import ExitStack

import concourse.mybir as mybir
from concourse.masks import make_identity

PIXELS, BASIS, WAVES, BANDS, CHANNELS = 2048, 512, 1024, 512, 1536
BLACK = 0.05
GAMMA = 1 / 2.2
FLOPS = 2 * (PIXELS * BASIS * WAVES + WAVES * BANDS * CHANNELS + PIXELS * WAVES * CHANNELS)

F32 = mybir.dt.float32
BF16 = mybir.dt.bfloat16
I32 = mybir.dt.int32
U32 = mybir.dt.uint32
U8 = mybir.dt.uint8
FP8X4 = mybir.dt.float8_e4m3fn_x4
FP4X4 = mybir.dt.float4_e2m1fn_x4
ALU = mybir.AluOpType
ACT = mybir.ActivationFunctionType

P = 128
SLOTS = 4
BANK = 512
GROUPS = WAVES // 512
TILES = PIXELS // P
CHUNKS = CHANNELS // BANK
FIRST_ROUND = 6
EARLY_TILES = 4
HELPED = 3
FINE = 2
LAST = [slice(0, 512), slice(512, 1024), slice(1024, 1536)]
HELPED_LATE = (13,)


def tile_spectral_camera_rendering_s12_kernel(
    tc, coef_words, coef_scales, spectra_words, spectra_scales, illum, sens, ccm, out
):
    nc = tc.nc
    with ExitStack() as ctx:
        keep = ctx.enter_context(tc.tile_pool(name="keep", bufs=1))
        psum = ctx.enter_context(tc.psum_pool(name="psum", bufs=4))
        ctx.enter_context(tc.manual_schedule())

        def kept(name, shape, dtype, tag=None, bufs=1):
            return keep.tile(shape, dtype, name=name, tag=tag or name, bufs=bufs, align_bytes=64)

        def bank(name, tag, shape, dtype=F32):
            return psum.tile(shape, dtype, name=name, tag=tag)

        spec_scale_raw = kept("spec_scale_raw", [P, WAVES], U8)
        coef_scale = kept("coef_scale", [P, PIXELS], U8)
        illum_rows = kept("illum_rows", [P, 2 * P], BF16)
        ident_f32 = kept("ident_f32", [P, P], F32)
        ident_bf16 = kept("ident_bf16", [P, P], BF16)
        nc.vector.memset(illum_rows[:], 0.0)
        nc.vector.memset(spec_scale_raw[:].bitcast(I32), 0)
        nc.vector.memset(coef_scale[:].bitcast(I32), 0)

        warm = kept("warm", [P, 8], F32)
        nc.vector.memset(warm[:], 1.0)
        nc.scalar.activation(out=warm[:], in_=warm[:], func=ACT.Ln)
        sens_raw = [kept("sens_raw%d" % k, [P, 2, BANDS], BF16) for k in range(4)]
        ccm_raw = [kept("ccm_raw%d" % c, [P, SLOTS, BANK], BF16) for c in range(CHUNKS)]
        spec_raw = kept("spec_raw", [P, 2 * WAVES], U8)
        coef_early = kept("coef_early", [P, 2 * P * EARLY_TILES], U8)
        coef_late = kept("coef_late", [P, 2 * P * (TILES - EARLY_TILES)], U8)

        def load_sens(k):
            g, h = divmod(k, 2)
            rows = sens[512 * g : 512 * (g + 1), :].rearrange("(p j) f -> p j f", j=4)
            nc.sync.dma_start(out=sens_raw[k][:], in_=rows[:, 2 * h : 2 * h + 2, :])

        def load_ccm(c):
            rows = ccm.rearrange("(p j) c -> p j c", j=SLOTS)
            nc.sync.dma_start(out=ccm_raw[c][:], in_=rows[:, :, BANK * c : BANK * (c + 1)])

        def load_scales(queue, plane, rows):
            for quad in range(4):
                queue.dma_start(
                    out=plane[32 * quad : 32 * quad + 4, :].bitcast(I32),
                    in_=rows[0, 4 * quad : 4 * quad + 4, :].bitcast(I32),
                )

        split = 2 * P * EARLY_TILES
        make_identity(nc, ident_bf16[:])
        make_identity(nc, ident_f32[:])
        nc.sync.dma_start(
            out=illum_rows[0:SLOTS, :].rearrange("t (b r) -> t b r", r=8),
            in_=illum.rearrange("(b t r) -> t b r", t=SLOTS, r=8),
        )
        load_scales(nc.gpsimd, spec_scale_raw, spectra_scales)
        load_sens(0)
        load_sens(1)
        load_ccm(0)
        load_sens(2)
        load_sens(3)
        load_ccm(1)
        nc.sync.dma_start(out=spec_raw[:].bitcast(I32), in_=spectra_words[0].bitcast(I32))
        nc.sync.dma_start(out=coef_early[:].bitcast(I32), in_=coef_words[0, :, 0:split].bitcast(I32))
        load_scales(nc.sync, coef_scale, coef_scales)
        load_ccm(2)
        nc.sync.dma_start(out=coef_late[:].bitcast(I32), in_=coef_words[0, :, split:].bitcast(I32))

        def quantize(name, source, tag=None, bufs=1):
            width = source.shape[1] // SLOTS
            codes = kept(name + "_codes", [P, width], U32, tag and tag + "_codes", bufs)
            scale = kept(name + "_scale", [P, width], U8, tag and tag + "_scale", bufs)
            nc.vector.quantize_mx(out=codes[:].bitcast(FP8X4), scales=scale[:], in_=source)
            return codes, scale

        sens_t = [kept("sens_t%d" % g, [P, SLOTS * 512], BF16) for g in range(GROUPS)]
        sens_mx = {}

        def turn_sens(k):
            g, h = divmod(k, 2)
            turned = bank("sens_bank%d" % k, "a", [P, 4, P])
            for j in range(2):
                words = sens_raw[k][:, j, :].bitcast(F32)
                for u in range(2):
                    nc.tensor.transpose(turned[:, 2 * j + u, :], words[:, u : 2 * P : 2], ident_f32[:])
            dst = sens_t[g][:].bitcast(F32).rearrange("p (t q a h x) -> p h t q a x", t=4, q=16, a=2, h=2)
            nc.scalar.copy(out=dst[:, h], in_=turned[:].rearrange("p x (q t a) -> p t q a x", t=4, a=2))

        def quantize_sens(g):
            sens_mx[g] = quantize("sens%d" % g, sens_t[g][:])

        ccm_il = {}
        ccm_mx = {}

        def interleave_ccm(c, copy):
            ccm_il[c] = kept("ccm_il%d" % c, [P, BANK * SLOTS], BF16)
            copy(
                out=ccm_il[c][:].rearrange("p (n i j) -> p n j i", i=4, j=SLOTS),
                in_=ccm_raw[c][:].rearrange("p j (n i) -> p n j i", i=4),
            )

        def quantize_ccm(c):
            ccm_mx[c] = quantize("ccm%d" % c, ccm_il[c][:])

        spec = kept("spec", [P, 2 * WAVES], U8)
        spec_scale = kept("spec_scale", [P, WAVES], U8)
        illum_full = kept("illum_full", [P, GROUPS, P, SLOTS], BF16)

        def order_spectra(dst, src):
            nc.vector.tensor_copy(
                out=dst[:].bitcast(I32).rearrange("p (g t q w) -> p g t q w", g=GROUPS, t=SLOTS, q=16),
                in_=src[:].bitcast(I32).rearrange("p (g q t w) -> p g t q w", g=GROUPS, t=SLOTS, q=16),
            )

        def spread_illum():
            turned = bank("illum_bank", "a", [P, GROUPS, P], BF16)
            for g in range(GROUPS):
                nc.tensor.transpose(turned[:, g, :], illum_rows[:, P * g : P * (g + 1)], ident_bf16[:])
            nc.scalar.copy(
                out=illum_full[:],
                in_=turned[:, :, 0:SLOTS].unsqueeze(2).to_broadcast([P, GROUPS, P, SLOTS]),
            )

        resp_bf = {}
        resp_mx = {}

        def resp_block(c, g, b):
            if b == 0:
                resp_bf[c, g] = kept("resp_bf%d_%d" % (c, g), [P, BANK * SLOTS], BF16, "resp_bf", 3)
            acc = bank("resp_bank%d_%d_%d" % (c, g, b), "a", [P, SLOTS, P])
            cols = slice(P * b, P * (b + 1))
            for t in range(SLOTS):
                waves = slice(P * t, P * (t + 1))
                nc.tensor.matmul_mx(
                    out=acc[:, t, :],
                    lhsT=sens_mx[g][0][:, waves].bitcast(FP8X4),
                    lhsT_scale=sens_mx[g][1][:, waves],
                    rhs=ccm_mx[c][0][:, cols].bitcast(FP8X4),
                    rhs_scale=ccm_mx[c][1][:, cols],
                    start=True,
                    stop=True,
                )
            dst = resp_bf[c, g][:, BANK * b : BANK * (b + 1)].rearrange("p (n t) -> p n t", t=SLOTS)
            nc.scalar.copy(out=dst, in_=acc[:].rearrange("p t n -> p n t"))

        def resp_group(c, g):
            for b in range(4):
                resp_block(c, g, b)

        def quantize_resp(c, g):
            resp_mx[c, g] = quantize("resp%d_%d" % (c, g), resp_bf[c, g][:])

        light_bf = {}
        light_mx = {}

        def light_group(i, g, tag):
            if g == 0:
                light_bf[i] = kept("light_bf%d" % i, [P, GROUPS, P, SLOTS], BF16, "light_bf", 3)
            acc = bank("refl_bank%d_%d" % (i, g), tag, [P, SLOTS, P])
            source, first = (coef_early, i) if i < EARLY_TILES else (coef_late, i - EARLY_TILES)
            for t in range(SLOTS):
                at = P * (SLOTS * g + t)
                nc.tensor.matmul_mx(
                    out=acc[:, t, :],
                    lhsT=spec[:, 2 * at : 2 * (at + P)].bitcast(FP4X4),
                    lhsT_scale=spec_scale[:, at : at + P],
                    rhs=source[:, 2 * P * first : 2 * P * (first + 1)].bitcast(FP4X4),
                    rhs_scale=coef_scale[:, P * i : P * (i + 1)],
                    start=(t == 0),
                    stop=(t == SLOTS - 1),
                )
            nc.vector.tensor_tensor(
                out=light_bf[i][:, g], in0=acc[:].rearrange("p t n -> p n t"), in1=illum_full[:, g], op=ALU.mult
            )

        def quantize_light(i):
            light_mx[i] = quantize("light%d" % i, light_bf[i][:].rearrange("p g n t -> p (g n t)"))

        result = [kept("result%d" % i, [P, CHANNELS], F32) for i in range(TILES)]

        def linear(i, c, on_scalar=False):
            acc = bank("lin_bank%d_%d" % (i, c), "a" if on_scalar else "b", [P, BANK])
            for g in range(GROUPS):
                nc.tensor.matmul_mx(
                    out=acc[:],
                    lhsT=light_mx[i][0][:, P * g : P * (g + 1)].bitcast(FP8X4),
                    lhsT_scale=light_mx[i][1][:, P * g : P * (g + 1)],
                    rhs=resp_mx[c, g][0][:].bitcast(FP8X4),
                    rhs_scale=resp_mx[c, g][1][:],
                    start=(g == 0),
                    stop=(g == GROUPS - 1),
                )
            dst = result[i][:, BANK * c : BANK * (c + 1)]
            if on_scalar:
                nc.scalar.activation(out=dst, in_=acc[:], func=ACT.Relu, bias=-BLACK)
            else:
                nc.vector.tensor_scalar(
                    out=dst, in0=acc[:], scalar1=BLACK, scalar2=0.0, op0=ALU.subtract, op1=ALU.max
                )

        def logarithm(i, cols):
            nc.scalar.activation(out=result[i][:, cols], in_=result[i][:, cols], func=ACT.Ln, bias=BLACK)

        def power(i, cols):
            nc.scalar.activation(out=result[i][:, cols], in_=result[i][:, cols], func=ACT.Exp, scale=GAMMA)
            nc.sync.dma_start(out=out[P * i : P * (i + 1), cols], in_=result[i][:, cols])

        whole = slice(0, CHANNELS)
        chunk = [slice(BANK * c, BANK * (c + 1)) for c in range(CHUNKS)]

        spread_illum()
        interleave_ccm(0, nc.vector.tensor_copy)
        turn_sens(0)
        turn_sens(1)
        turn_sens(2)
        turn_sens(3)
        quantize_sens(0)
        quantize_ccm(0)
        resp_group(0, 0)
        interleave_ccm(1, nc.vector.tensor_copy)
        quantize_sens(1)
        order_spectra(spec_scale, spec_scale_raw)
        order_spectra(spec, spec_raw)
        quantize_ccm(1)
        light_group(0, 0, "b")
        light_group(0, 1, "b")
        resp_group(0, 1)
        interleave_ccm(2, nc.vector.tensor_copy)
        quantize_light(0)
        quantize_resp(0, 0)
        quantize_ccm(2)
        pending = [(c, g) for c in range(CHUNKS) for g in range(GROUPS)]
        for i in range(1, FIRST_ROUND):
            light_group(i, 0, "b")
            light_group(i, 1, "b")
            if i + 1 < len(pending):
                resp_group(*pending[i + 1])
            else:
                for j in range(HELPED):
                    linear(j, 0, True)
            quantize_resp(*pending[i])
            quantize_light(i)
        for c in range(CHUNKS):
            for i in range(FIRST_ROUND):
                if c > 0 or i >= HELPED:
                    linear(i, c)
                logarithm(i, chunk[c])
        light_group(FIRST_ROUND, 0, "b")
        light_group(FIRST_ROUND, 1, "b")
        light_group(FIRST_ROUND + 1, 0, "b")
        quantize_light(FIRST_ROUND)
        light_group(FIRST_ROUND + 1, 1, "b")
        for i in range(FIRST_ROUND):
            power(i, whole)
        for i in range(FIRST_ROUND, TILES):
            if i + 2 < TILES:
                light_group(i + 2, 0, "a")
            linear(i, 0)
            if i + 1 < TILES:
                quantize_light(i + 1)
            if i + 2 < TILES:
                light_group(i + 2, 1, "a")
            linear(i, 1)
            linear(i, 2, i in HELPED_LATE)
            for cols in chunk if i >= TILES - FINE else [whole]:
                logarithm(i, cols)
        for i in range(FIRST_ROUND, TILES):
            for cols in chunk if i == FIRST_ROUND else (LAST if i == TILES - 1 else [whole]):
                power(i, cols)
